import numpy as np
import ml_dtypes


def mxq(x, axis, fmt="e4m3"):
    dtype, down = {"e4m3": (ml_dtypes.float8_e4m3fn, 7), "e5m2": (ml_dtypes.float8_e5m2, 14)}[fmt]
    v = np.moveaxis(np.asarray(x, np.float32).astype(ml_dtypes.bfloat16).astype(np.float64), axis, -1)
    blocks = v.reshape(v.shape[:-1] + (-1, 32))
    amax = np.abs(blocks).max(-1, keepdims=True)
    byte = np.maximum(np.where(amax > 0, np.frexp(amax)[1] - 1 + 127, 0) - down, 1)
    scale = np.exp2(byte - 127.0)
    codes = (blocks / scale).astype(np.float32).astype(dtype).astype(np.float64)
    return np.moveaxis((codes * scale).reshape(v.shape), -1, axis)


WIDE = False


def mx_kscale(k):
    if not WIDE:
        return np.ones(k)
    levels = np.array([10, -10, 5, -5, 0])
    if k % 512:
        return np.exp2(np.random.permutation(np.resize(levels, k // 32))).repeat(32)
    a = np.empty((k // 512, 16))
    for p in range(k // 512):
        a[p, :8] = np.random.permutation(np.resize(levels, 8))
        for g in range(8):
            far = levels[np.abs(levels - a[p, g]) >= 10]
            a[p, g + 8] = far[np.random.randint(len(far))]
    return np.exp2(a.ravel()).repeat(32)


def f64(x):
    return np.asarray(x).astype(np.float64)


def striped(idx):
    return np.tile(np.asarray(idx).reshape(-1, 16).T, (8, 1)).astype(np.uint16)


def unstriped(offs):
    return offs[:16].T.reshape(-1).astype(np.int64)


E2M1 = np.array([0.0, 0.5, 1.0, 1.5, 2.0, 3.0, 4.0, 6.0, -0.0, -0.5, -1.0, -1.5, -2.0, -3.0, -4.0, -6.0])


def pack_weight(w, fmt):
    k, n = w.shape
    w = f64(np.asarray(w, np.float32).astype(ml_dtypes.bfloat16)).reshape(k // 32, 32, n)
    amax = np.abs(w).max(1)
    if fmt == "e4m3":
        byte = np.frexp(amax)[1] - 1 + 127 - 7
    else:
        mant, ex = np.frexp(amax / 6.0)
        byte = np.where(mant > 0.5, ex, ex - 1) + 127
    byte = np.clip(np.where(amax > 0, byte, 1), 1, 254)
    scaled = (w * np.exp2(127.0 - byte)[:, None, :]).reshape(k, n).astype(np.float32)
    by_word = np.ascontiguousarray(scaled.reshape(k // 512, 128, 4, n).transpose(0, 1, 3, 2))
    if fmt == "e4m3":
        words = by_word.astype(ml_dtypes.float8_e4m3fn).view(np.uint8)
    else:
        c = by_word.astype(ml_dtypes.float4_e2m1fn).view(np.uint8) & 0xF
        words = (c[..., 0::2] | (c[..., 1::2] << 4)).reshape(k // 512, 128, 2 * n)
    return np.ascontiguousarray(words), np.ascontiguousarray(byte.astype(np.uint8).reshape(k // 512, 16, n))


def unpack_weight(words, scales, fmt):
    g, _, n = scales.shape
    words = np.ascontiguousarray(words).reshape(g, 128, n, -1)
    if fmt == "e4m3":
        vals = words.view(ml_dtypes.float8_e4m3fn).astype(np.float64)
    else:
        nib = np.empty((g, 128, n, 4), np.uint8)
        nib[..., 0::2] = words & 0xF
        nib[..., 1::2] = words >> 4
        vals = E2M1[nib]
    vals = vals * np.repeat(np.exp2(scales.astype(np.float64) - 127.0), 8, axis=1)[..., None]
    return vals.transpose(0, 1, 3, 2).reshape(g * 512, n)


K, T, J, N = 512, 2048, 512, 512


def setup_inputs():
    n = np.random.standard_normal
    idx = np.random.permutation(T)[:J]
    idx2 = np.random.permutation(T)[:J]
    fj = mx_kscale(J)
    tgp = pack_weight(n((J, N)) * fj[:, None], "e4m3")
    return {
        "xf": (n((K, T))).astype(np.float32),
        "rw": (np.random.uniform(0.5, 2.0, (1, J)) / fj).astype(np.float32),
        "tg_words": tgp[0],
        "tg_scales": tgp[1],
        "old": (1.0 * n((K, N))).astype(np.float32),
        "offs": striped(idx),
        "offs2": striped(idx2),
    }


def reference(xf, rw, tg_words, tg_scales, old, offs, offs2):
    idx = unstriped(offs)
    idx2 = unstriped(offs2)
    tgu = unpack_weight(tg_words, tg_scales, "e4m3")
    d = (f64(xf)[:, idx] - f64(xf)[:, idx2]) * f64(rw)
    dt1 = d.T
    dt1q = mxq(dt1, 0, "e4m3")
    w = dt1q.T @ tgu
    y = 0.03 * w + 0.5 * f64(old)
    return y

@@ -1,0 +1,153 @@
+from contextlib import ExitStack
+
+import concourse.mybir as mybir
+from concourse.masks import make_identity
+
+K, T, J, N = 512, 2048, 512, 512
+FLOPS = 2 * K * J * N
+
+F32 = mybir.dt.float32
+BF16 = mybir.dt.bfloat16
+I32 = mybir.dt.int32
+U32 = mybir.dt.uint32
+U16 = mybir.dt.uint16
+U8 = mybir.dt.uint8
+FP8X4 = mybir.dt.float8_e4m3fn_x4
+COPY = mybir.ActivationFunctionType.Copy
+MULT = mybir.AluOpType.mult
+ADD = mybir.AluOpType.add
+SUB = mybir.AluOpType.subtract
+
+P = 128
+PACK = 4
+TILES = K // P
+HALF = J // 2
+
+
+def tile_list_moment_of_changes_kernel(tc, xf, rw, tg_words, tg_scales, old, offs, offs2, out):
+    nc = tc.nc
+    with ExitStack() as ctx:
+        held = ctx.enter_context(tc.tile_pool(name="held", bufs=1))
+        psum = ctx.enter_context(tc.psum_pool(name="psum", bufs=1))
+
+        list1 = held.tile([P, J // 16], U16, name="list1")
+        list2 = held.tile([P, J // 16], U16, name="list2")
+        x = [held.tile([P, T], F32, name=f"x{i}") for i in range(TILES)]
+        old_sb = held.tile([P, TILES, N], F32, name="old_sb")
+        rw_sb = held.tile([P, PACK], F32, name="rw_sb")
+        tg_codes = held.tile([P, N], U32, name="tg_codes", align_bytes=64)
+        tg_plane = held.tile([P, N], U8, name="tg_plane", align_bytes=64)
+        ident = held.tile([P, P], F32, name="ident")
+
+        xf_rows = xf.rearrange("(p i) t -> i p t", i=TILES)
+        out_rows = out.rearrange("(p i) n -> i p n", i=TILES)
+        nc.gpsimd.memset(tg_plane[:].bitcast(I32), 0)
+        nc.sync.dma_start(x[0][:], xf_rows[0])
+        nc.sync.dma_start(list2[:], offs2)
+        nc.sync.dma_start(list1[:], offs)
+        nc.sync.dma_start(rw_sb[:], rw.rearrange("o (p t) -> (o p) t", t=PACK))
+        nc.sync.dma_start(x[1][:], xf_rows[1])
+        for q in range(4):
+            nc.sync.dma_start(
+                tg_plane[32 * q : 32 * q + 4, :].bitcast(I32),
+                tg_scales[0, 4 * q : 4 * q + 4, :].bitcast(I32),
+            )
+        nc.sync.dma_start(
+            tg_codes[:].bitcast(I32), tg_words[0].rearrange("p n t -> p (n t)").bitcast(I32)
+        )
+        for i in range(2, TILES):
+            nc.sync.dma_start(x[i][:], xf_rows[i])
+        nc.sync.dma_start(old_sb[:], old.rearrange("(p i) n -> p i n", i=TILES))
+        make_identity(nc, ident[:])
+
+        diff, grouped, codes, plane, acc, half_old = {}, {}, {}, {}, {}, {}
+
+        def gather(i):
+            second = held.tile([P, J], F32, name=f"second{i}", tag=f"slot{i}", align_bytes=64)
+            diff[i] = held.tile([P, J], F32, name=f"diff{i}")
+            for h in range(2):
+                nc.vector.tensor_copy(
+                    second[:, h * HALF : (h + 1) * HALF],
+                    x[i][:].indirect(list2[:, h * 16 : (h + 1) * 16]),
+                )
+            for h in range(2):
+                nc.vector.tensor_tensor(
+                    diff[i][:, h * HALF : (h + 1) * HALF],
+                    x[i][:].indirect(list1[:, h * 16 : (h + 1) * 16]),
+                    second[:, h * HALF : (h + 1) * HALF],
+                    SUB,
+                )
+
+        def turn_on_scalar(i):
+            grouped[i] = held.tile([P, P, PACK], BF16, name=f"grouped{i}", tag=f"grouped{i}", align_bytes=64)
+            for t in range(PACK):
+                bank = psum.tile([P, P], F32, name=f"turned{i}_{t}", tag=f"turn{t}")
+                nc.tensor.transpose(bank[:], diff[i][:, t::PACK], ident[:])
+                nc.scalar.activation(grouped[i][:, :, t], bank[:], COPY, scale=rw_sb[:, t : t + 1])
+
+        def turn_last(i):
+            bank = psum.tile([P, PACK, P], F32, name=f"turned{i}", tag="turn0")
+            for t in range(PACK):
+                nc.tensor.transpose(bank[:, t, :], diff[i][:, t::PACK], ident[:])
+            return bank
+
+        def weigh_last(i, bank):
+            grouped[i] = held.tile([P, P, PACK], BF16, name=f"grouped{i}", tag=f"grouped{i}", align_bytes=64)
+            nc.vector.tensor_tensor(
+                grouped[i][:],
+                bank[:].rearrange("p t k -> p k t"),
+                rw_sb[:].unsqueeze(1).to_broadcast([P, P, PACK]),
+                MULT,
+            )
+
+        def quantise(i):
+            codes[i] = held.tile([P, P], U32, name=f"codes{i}", tag=f"slot{i + 1}", align_bytes=64)
+            plane[i] = held.tile([P, P], U8, name=f"plane{i}", align_bytes=64)
+            nc.vector.quantize_mx(
+                out=codes[i][:].bitcast(FP8X4),
+                scales=plane[i][:],
+                in_=grouped[i][:].rearrange("p k t -> p (k t)"),
+            )
+
+        def multiply(i):
+            acc[i] = psum.tile([P, N], F32, name=f"acc{i}")
+            nc.tensor.matmul_mx(
+                out=acc[i][:],
+                lhsT=codes[i][:].bitcast(FP8X4),
+                lhsT_scale=plane[i][:],
+                rhs=tg_codes[:].bitcast(FP8X4),
+                rhs_scale=tg_plane[:],
+                start=True,
+                stop=True,
+            )
+
+        def halve(i):
+            half_old[i] = held.tile([P, N], F32, name=f"half_old{i}")
+            nc.scalar.activation(half_old[i][:], old_sb[:, i, :], COPY, scale=0.5)
+
+        def finish(i, tag):
+            y = held.tile([P, N], F32, name=f"y{i}", tag=tag, align_bytes=64)
+            nc.vector.scalar_tensor_tensor(y[:], acc[i][:], 0.03, half_old[i][:], MULT, ADD)
+            nc.sync.dma_start(out_rows[i], y[:])
+
+        last = TILES - 1
+        gather(0)
+        turn_on_scalar(0)
+        for i in range(1, last):
+            gather(i)
+            turn_on_scalar(i)
+            quantise(i - 1)
+            multiply(i - 1)
+        gather(last)
+        bank_last = turn_last(last)
+        quantise(last - 1)
+        multiply(last - 1)
+        for i in range(TILES):
+            halve(i)
+        finish(0, "y0")
+        finish(1, "y1")
+        weigh_last(last, bank_last)
+        quantise(last)
+        multiply(last)
+        finish(2, f"grouped{last}")
+        finish(last, "y3")

@@ -32,8 +32,8 @@ def tile_list_moment_of_changes_kernel(tc, xf, rw, tg_words, tg_scales, old, off
 
         list1 = held.tile([P, J // 16], U16, name="list1")
         list2 = held.tile([P, J // 16], U16, name="list2")
-        x = [held.tile([P, T], F32, name=f"x{i}") for i in range(TILES)]
-        old_sb = held.tile([P, TILES, N], F32, name="old_sb")
+        x = [held.tile([P, T], F32, name=f"x{i}", tag=f"slot{i}", align_bytes=64) for i in range(TILES)]
+        old_sb = [held.tile([P, 2, N], F32, name=f"old{h}", tag=f"old{h}", align_bytes=64) for h in range(2)]
         rw_sb = held.tile([P, PACK], F32, name="rw_sb")
         tg_codes = held.tile([P, N], U32, name="tg_codes", align_bytes=64)
         tg_plane = held.tile([P, N], U8, name="tg_plane", align_bytes=64)
@@ -57,42 +57,40 @@ def tile_list_moment_of_changes_kernel(tc, xf, rw, tg_words, tg_scales, old, off
         )
         for i in range(2, TILES):
             nc.sync.dma_start(x[i][:], xf_rows[i])
-        nc.sync.dma_start(old_sb[:], old.rearrange("(p i) n -> p i n", i=TILES))
+        for h in range(2):
+            nc.sync.dma_start(old_sb[h][:], old.rearrange("(p i) n -> p i n", i=TILES)[:, 2 * h : 2 * h + 2, :])
         make_identity(nc, ident[:])
 
-        diff, grouped, codes, plane, acc, half_old = {}, {}, {}, {}, {}, {}
+        minus, plus, grouped, codes, plane, acc, half_old = {}, {}, {}, {}, {}, {}, {}
 
         def gather(i):
-            second = held.tile([P, J], F32, name=f"second{i}", tag=f"slot{i}", align_bytes=64)
-            diff[i] = held.tile([P, J], F32, name=f"diff{i}")
-            for h in range(2):
-                nc.vector.tensor_copy(
-                    second[:, h * HALF : (h + 1) * HALF],
-                    x[i][:].indirect(list2[:, h * 16 : (h + 1) * 16]),
-                )
-            for h in range(2):
-                nc.vector.tensor_tensor(
-                    diff[i][:, h * HALF : (h + 1) * HALF],
-                    x[i][:].indirect(list1[:, h * 16 : (h + 1) * 16]),
-                    second[:, h * HALF : (h + 1) * HALF],
-                    SUB,
-                )
+            minus[i] = held.tile([P, J], F32, name=f"minus{i}")
+            plus[i] = held.tile([P, J], F32, name=f"plus{i}")
+            nc.vector.tensor_scalar(minus[i][:], x[i][:].indirect(list2[:]), -1.0, 0.0, MULT, ADD)
+            nc.vector.tensor_copy(plus[i][:], x[i][:].indirect(list1[:]))
+
+        def turn(dst, src, t, start, stop):
+            nc.tensor.matmul(dst, src[:, t::PACK], ident[:], start=start, stop=stop, is_transpose=True)
 
         def turn_on_scalar(i):
             grouped[i] = held.tile([P, P, PACK], BF16, name=f"grouped{i}", tag=f"grouped{i}", align_bytes=64)
+            banks = [psum.tile([P, P], F32, name=f"turned{i}_{t}", tag="ring", bufs=6) for t in range(PACK)]
             for t in range(PACK):
-                bank = psum.tile([P, P], F32, name=f"turned{i}_{t}", tag=f"turn{t}")
-                nc.tensor.transpose(bank[:], diff[i][:, t::PACK], ident[:])
-                nc.scalar.activation(grouped[i][:, :, t], bank[:], COPY, scale=rw_sb[:, t : t + 1])
+                turn(banks[t][:], minus[i], t, True, False)
+            for t in range(PACK):
+                turn(banks[t][:], plus[i], t, False, True)
+                nc.scalar.activation(grouped[i][:, :, t], banks[t][:], COPY, scale=rw_sb[:, t : t + 1])
 
         def turn_last(i):
-            bank = psum.tile([P, PACK, P], F32, name=f"turned{i}", tag="turn0")
+            bank = psum.tile([P, PACK, P], F32, name=f"turned{i}", tag="ring", bufs=6)
             for t in range(PACK):
-                nc.tensor.transpose(bank[:, t, :], diff[i][:, t::PACK], ident[:])
+                turn(bank[:, t, :], minus[i], t, t == 0, False)
+            for t in range(PACK):
+                turn(bank[:, t, :], plus[i], t, False, t == PACK - 1)
             return bank
 
         def weigh_last(i, bank):
-            grouped[i] = held.tile([P, P, PACK], BF16, name=f"grouped{i}", tag=f"grouped{i}", align_bytes=64)
+            grouped[i] = held.tile([P, P, PACK], BF16, name=f"grouped{i}", tag="old0", align_bytes=64)
             nc.vector.tensor_tensor(
                 grouped[i][:],
                 bank[:].rearrange("p t k -> p k t"),
@@ -110,7 +108,10 @@ def tile_list_moment_of_changes_kernel(tc, xf, rw, tg_words, tg_scales, old, off
             )
 
         def multiply(i):
-            acc[i] = psum.tile([P, N], F32, name=f"acc{i}")
+            if i < 2:
+                acc[i] = psum.tile([P, N], F32, name=f"acc{i}")
+            else:
+                acc[i] = psum.tile([P, N], F32, name=f"acc{i}", tag="ring", bufs=6)
             nc.tensor.matmul_mx(
                 out=acc[i][:],
                 lhsT=codes[i][:].bitcast(FP8X4),
@@ -123,11 +124,18 @@ def tile_list_moment_of_changes_kernel(tc, xf, rw, tg_words, tg_scales, old, off
 
         def halve(i):
             half_old[i] = held.tile([P, N], F32, name=f"half_old{i}")
-            nc.scalar.activation(half_old[i][:], old_sb[:, i, :], COPY, scale=0.5)
+            nc.scalar.activation(half_old[i][:], old_sb[i // 2][:, i % 2, :], COPY, scale=0.5)
 
         def finish(i, tag):
             y = held.tile([P, N], F32, name=f"y{i}", tag=tag, align_bytes=64)
             nc.vector.scalar_tensor_tensor(y[:], acc[i][:], 0.03, half_old[i][:], MULT, ADD)
+            nc.sync.dma_start(out_rows[i], y[:])
+
+        def finish_early(i):
+            twice = held.tile([P, N], F32, name=f"twice{i}")
+            y = held.tile([P, N], F32, name=f"y{i}")
+            nc.vector.scalar_tensor_tensor(twice[:], acc[i][:], 0.06, old_sb[0][:, i, :], MULT, ADD)
+            nc.scalar.activation(y[:], twice[:], COPY, scale=0.5)
             nc.sync.dma_start(out_rows[i], y[:])
 
         last = TILES - 1
@@ -142,12 +150,12 @@ def tile_list_moment_of_changes_kernel(tc, xf, rw, tg_words, tg_scales, old, off
         bank_last = turn_last(last)
         quantise(last - 1)
         multiply(last - 1)
-        for i in range(TILES):
-            halve(i)
-        finish(0, "y0")
-        finish(1, "y1")
+        halve(2)
+        halve(3)
+        finish_early(0)
+        finish_early(1)
         weigh_last(last, bank_last)
         quantise(last)
         multiply(last)
-        finish(2, f"grouped{last}")
+        finish(2, "old0")
         finish(last, "y3")

@@ -26,20 +26,22 @@ HALF = J // 2
 
 def tile_list_moment_of_changes_kernel(tc, xf, rw, tg_words, tg_scales, old, offs, offs2, out):
     nc = tc.nc
+    last = TILES - 1
     with ExitStack() as ctx:
         held = ctx.enter_context(tc.tile_pool(name="held", bufs=1))
         psum = ctx.enter_context(tc.psum_pool(name="psum", bufs=1))
 
         list1 = held.tile([P, J // 16], U16, name="list1")
         list2 = held.tile([P, J // 16], U16, name="list2")
-        x = [held.tile([P, T], F32, name=f"x{i}", tag=f"slot{i}", align_bytes=64) for i in range(TILES)]
-        old_sb = [held.tile([P, 2, N], F32, name=f"old{h}", tag=f"old{h}", align_bytes=64) for h in range(2)]
+        x = [held.tile([P, T], F32, name=f"x{i}", tag=f"window{i}", align_bytes=64) for i in range(TILES)]
+        old_sb = [held.tile([P, N], F32, name=f"old{i}", tag=f"old{i}", align_bytes=64) for i in range(TILES)]
         rw_sb = held.tile([P, PACK], F32, name="rw_sb")
         tg_codes = held.tile([P, N], U32, name="tg_codes", align_bytes=64)
         tg_plane = held.tile([P, N], U8, name="tg_plane", align_bytes=64)
         ident = held.tile([P, P], F32, name="ident")
 
         xf_rows = xf.rearrange("(p i) t -> i p t", i=TILES)
+        old_rows = old.rearrange("(p i) n -> p i n", i=TILES)
         out_rows = out.rearrange("(p i) n -> i p n", i=TILES)
         nc.gpsimd.memset(tg_plane[:].bitcast(I32), 0)
         nc.sync.dma_start(x[0][:], xf_rows[0])
@@ -52,110 +54,106 @@ def tile_list_moment_of_changes_kernel(tc, xf, rw, tg_words, tg_scales, old, off
                 tg_plane[32 * q : 32 * q + 4, :].bitcast(I32),
                 tg_scales[0, 4 * q : 4 * q + 4, :].bitcast(I32),
             )
+        for i in range(2, TILES):
+            nc.sync.dma_start(x[i][:], xf_rows[i])
         nc.sync.dma_start(
             tg_codes[:].bitcast(I32), tg_words[0].rearrange("p n t -> p (n t)").bitcast(I32)
         )
-        for i in range(2, TILES):
-            nc.sync.dma_start(x[i][:], xf_rows[i])
-        for h in range(2):
-            nc.sync.dma_start(old_sb[h][:], old.rearrange("(p i) n -> p i n", i=TILES)[:, 2 * h : 2 * h + 2, :])
+        for i in range(TILES):
+            nc.sync.dma_start(old_sb[i][:], old_rows[:, i, :])
         make_identity(nc, ident[:])
 
-        minus, plus, grouped, codes, plane, acc, half_old = {}, {}, {}, {}, {}, {}, {}
+        rw_wide = psum.tile([P, PACK, P], F32, name="rw_wide", tag="shared")
+        for t in range(PACK):
+            nc.tensor.transpose(rw_wide[:, t, :], rw_sb[:, t : t + 1].to_broadcast([P, P]), ident[:])
 
-        def gather(i):
-            minus[i] = held.tile([P, J], F32, name=f"minus{i}")
-            plus[i] = held.tile([P, J], F32, name=f"plus{i}")
-            nc.vector.tensor_scalar(minus[i][:], x[i][:].indirect(list2[:]), -1.0, 0.0, MULT, ADD)
-            nc.vector.tensor_copy(plus[i][:], x[i][:].indirect(list1[:]))
-
-        def turn(dst, src, t, start, stop):
-            nc.tensor.matmul(dst, src[:, t::PACK], ident[:], start=start, stop=stop, is_transpose=True)
-
-        def turn_on_scalar(i):
-            grouped[i] = held.tile([P, P, PACK], BF16, name=f"grouped{i}", tag=f"grouped{i}", align_bytes=64)
-            banks = [psum.tile([P, P], F32, name=f"turned{i}_{t}", tag="ring", bufs=6) for t in range(PACK)]
+        def gather_and_turn(i, grouped):
+            minus = held.tile([P, J], F32, name=f"minus{i}")
+            plus = held.tile([P, J], F32, name=f"plus{i}")
+            nc.vector.tensor_scalar(minus[:], x[i][:].indirect(list2[:]), -1.0, 0.0, MULT, ADD)
+            nc.vector.tensor_copy(plus[:], x[i][:].indirect(list1[:]))
+            banks = [psum.tile([P, P], F32, name=f"turned{i}_{t}", tag="ring", bufs=5) for t in range(PACK)]
             for t in range(PACK):
-                turn(banks[t][:], minus[i], t, True, False)
+                nc.tensor.matmul(banks[t][:], minus[:, t::PACK], ident[:], start=True, stop=False, is_transpose=True)
             for t in range(PACK):
-                turn(banks[t][:], plus[i], t, False, True)
-                nc.scalar.activation(grouped[i][:, :, t], banks[t][:], COPY, scale=rw_sb[:, t : t + 1])
+                nc.tensor.matmul(banks[t][:], plus[:, t::PACK], ident[:], start=False, stop=True, is_transpose=True)
+                nc.scalar.activation(grouped[:, :, t], banks[t][:], COPY, scale=rw_sb[:, t : t + 1])
 
-        def turn_last(i):
-            bank = psum.tile([P, PACK, P], F32, name=f"turned{i}", tag="ring", bufs=6)
-            for t in range(PACK):
-                turn(bank[:, t, :], minus[i], t, t == 0, False)
-            for t in range(PACK):
-                turn(bank[:, t, :], plus[i], t, False, t == PACK - 1)
-            return bank
+        def quantise(name, grouped, width, tag):
+            codes = held.tile([P, width], U32, name=f"codes{name}", tag=tag, align_bytes=64)
+            plane = held.tile([P, width], U8, name=f"plane{name}", align_bytes=64)
+            nc.vector.quantize_mx(out=codes[:].bitcast(FP8X4), scales=plane[:], in_=grouped)
+            return codes, plane
 
-        def weigh_last(i, bank):
-            grouped[i] = held.tile([P, P, PACK], BF16, name=f"grouped{i}", tag="old0", align_bytes=64)
-            nc.vector.tensor_tensor(
-                grouped[i][:],
-                bank[:].rearrange("p t k -> p k t"),
-                rw_sb[:].unsqueeze(1).to_broadcast([P, P, PACK]),
-                MULT,
-            )
-
-        def quantise(i):
-            codes[i] = held.tile([P, P], U32, name=f"codes{i}", tag=f"slot{i + 1}", align_bytes=64)
-            plane[i] = held.tile([P, P], U8, name=f"plane{i}", align_bytes=64)
-            nc.vector.quantize_mx(
-                out=codes[i][:].bitcast(FP8X4),
-                scales=plane[i][:],
-                in_=grouped[i][:].rearrange("p k t -> p (k t)"),
-            )
-
-        def multiply(i):
-            if i < 2:
-                acc[i] = psum.tile([P, N], F32, name=f"acc{i}")
-            else:
-                acc[i] = psum.tile([P, N], F32, name=f"acc{i}", tag="ring", bufs=6)
+        def multiply(acc, quantised, k_cols, n_cols):
+            codes, plane = quantised
             nc.tensor.matmul_mx(
-                out=acc[i][:],
-                lhsT=codes[i][:].bitcast(FP8X4),
-                lhsT_scale=plane[i][:],
-                rhs=tg_codes[:].bitcast(FP8X4),
-                rhs_scale=tg_plane[:],
+                out=acc[:],
+                lhsT=codes[:, k_cols].bitcast(FP8X4),
+                lhsT_scale=plane[:, k_cols],
+                rhs=tg_codes[:, n_cols].bitcast(FP8X4),
+                rhs_scale=tg_plane[:, n_cols],
                 start=True,
                 stop=True,
             )
 
         def halve(i):
-            half_old[i] = held.tile([P, N], F32, name=f"half_old{i}")
-            nc.scalar.activation(half_old[i][:], old_sb[i // 2][:, i % 2, :], COPY, scale=0.5)
+            half = held.tile([P, N], F32, name=f"half{i}", tag=f"half{i}", align_bytes=64)
+            nc.scalar.activation(half[:], old_sb[i][:], COPY, scale=0.5)
+            return half
 
-        def finish(i, tag):
-            y = held.tile([P, N], F32, name=f"y{i}", tag=tag, align_bytes=64)
-            nc.vector.scalar_tensor_tensor(y[:], acc[i][:], 0.03, half_old[i][:], MULT, ADD)
-            nc.sync.dma_start(out_rows[i], y[:])
+        def finish(i, acc, n_cols, name, tag, queue):
+            y = held.tile([P, n_cols.stop - n_cols.start], F32, name=name, tag=tag, align_bytes=64)
+            nc.vector.scalar_tensor_tensor(y[:], acc[:], 0.03, half_old[i][:, n_cols], MULT, ADD)
+            queue.dma_start(out_rows[i][:, n_cols], y[:])
 
-        def finish_early(i):
-            twice = held.tile([P, N], F32, name=f"twice{i}")
-            y = held.tile([P, N], F32, name=f"y{i}")
-            nc.vector.scalar_tensor_tensor(twice[:], acc[i][:], 0.06, old_sb[0][:, i, :], MULT, ADD)
-            nc.scalar.activation(y[:], twice[:], COPY, scale=0.5)
-            nc.sync.dma_start(out_rows[i], y[:])
+        all_n = slice(0, N)
+        first_k = slice(0, P)
+        grouped01 = held.tile([P, 2, P, PACK], BF16, name="grouped01", align_bytes=64)
+        grouped2 = held.tile([P, P, PACK], BF16, name="grouped2", align_bytes=64)
+        gather_and_turn(0, grouped01[:, 0])
+        gather_and_turn(1, grouped01[:, 1])
+        gather_and_turn(2, grouped2[:])
+        quantised01 = quantise("01", grouped01[:].rearrange("p i k t -> p (i k t)"), 2 * P, "window2")
+        acc01 = [psum.tile([P, N], F32, name=f"acc{i}") for i in range(2)]
+        for i in range(2):
+            multiply(acc01[i], quantised01, slice(i * P, (i + 1) * P), all_n)
 
-        last = TILES - 1
-        gather(0)
-        turn_on_scalar(0)
-        for i in range(1, last):
-            gather(i)
-            turn_on_scalar(i)
-            quantise(i - 1)
-            multiply(i - 1)
-        gather(last)
-        bank_last = turn_last(last)
-        quantise(last - 1)
-        multiply(last - 1)
-        halve(2)
-        halve(3)
-        finish_early(0)
-        finish_early(1)
-        weigh_last(last, bank_last)
-        quantise(last)
-        multiply(last)
-        finish(2, "old0")
-        finish(last, "y3")
+        second = held.tile([P, J], F32, name="second")
+        diff = held.tile([P, J], F32, name="diff")
+        pairs = held.tile([P, 2, J // 2], BF16, name="pairs", align_bytes=64)
+        halves = [slice(h * HALF, (h + 1) * HALF) for h in range(2)]
+        for h in range(2):
+            nc.vector.tensor_copy(second[:, halves[h]], x[last][:].indirect(list2[:, h * 16 : (h + 1) * 16]))
+        for h in range(2):
+            nc.vector.tensor_tensor(
+                diff[:, halves[h]], x[last][:].indirect(list1[:, h * 16 : (h + 1) * 16]), second[:, halves[h]], SUB
+            )
+        for h in range(2):
+            q_cols = slice(h * 64, (h + 1) * 64)
+            nc.vector.tensor_tensor(
+                pairs[:].rearrange("p u (q e) -> p u q e", e=2)[:, :, q_cols, :],
+                diff[:, halves[h]].rearrange("p (q u e) -> p u q e", u=2, e=2),
+                rw_wide[:].rearrange("p (u e) q -> p u q e", e=2)[:, :, q_cols, :],
+                MULT,
+            )
+        turned = psum.tile([P, 2, P], F32, name="turned_pairs", tag="shared")
+        for u in range(2):
+            nc.tensor.transpose(turned[:, u, :], pairs[:].bitcast(F32)[:, u, :], ident[:])
+        half_old = [halve(i) for i in range(2)]
+        grouped3 = held.tile([P, P, PACK], BF16, name="grouped3", tag="old1", align_bytes=64)
+        nc.scalar.copy(grouped3[:].bitcast(F32), turned[:].rearrange("p u k -> p k u"))
+        half_old.extend(halve(i) for i in range(2, TILES))
+
+        quantised2 = quantise("2", grouped2[:].rearrange("p k t -> p (k t)"), P, "window3")
+        acc2 = psum.tile([P, N], F32, name="acc2", tag="ring", bufs=5)
+        multiply(acc2, quantised2, first_k, all_n)
+        finish(0, acc01[0], all_n, "y0", "y0", nc.sync)
+        finish(1, acc01[1], all_n, "y1", "y1", nc.sync)
+        quantised3 = quantise("3", grouped3[:].rearrange("p k t -> p (k t)"), P, "half0")
+        acc3 = [psum.tile([P, N // 2], F32, name=f"acc3_{h}", tag="ring", bufs=5) for h in range(2)]
+        for h in range(2):
+            multiply(acc3[h], quantised3, first_k, halves[h])
+        finish(2, acc2, all_n, "y2", "old1", nc.sync)
+        finish(last, acc3[0], halves[0], "y3a", "y3a", nc.sync)
+        finish(last, acc3[1], halves[1], "y3b", "y3b", nc.scalar)

@@ -22,6 +22,7 @@ P = 128
 PACK = 4
 TILES = K // P
 HALF = J // 2
+RING = 7
 
 
 def tile_list_moment_of_changes_kernel(tc, xf, rw, tg_words, tg_scales, old, offs, offs2, out):
@@ -43,19 +44,23 @@ def tile_list_moment_of_changes_kernel(tc, xf, rw, tg_words, tg_scales, old, off
         xf_rows = xf.rearrange("(p i) t -> i p t", i=TILES)
         old_rows = old.rearrange("(p i) n -> p i n", i=TILES)
         out_rows = out.rearrange("(p i) n -> i p n", i=TILES)
+        def load_scales(q):
+            nc.sync.dma_start(
+                tg_plane[32 * q : 32 * q + 4, :].bitcast(I32),
+                tg_scales[0, 4 * q : 4 * q + 4, :].bitcast(I32),
+            )
+
         nc.gpsimd.memset(tg_plane[:].bitcast(I32), 0)
         nc.sync.dma_start(x[0][:], xf_rows[0])
         nc.sync.dma_start(list2[:], offs2)
         nc.sync.dma_start(list1[:], offs)
         nc.sync.dma_start(rw_sb[:], rw.rearrange("o (p t) -> (o p) t", t=PACK))
         nc.sync.dma_start(x[1][:], xf_rows[1])
-        for q in range(4):
-            nc.sync.dma_start(
-                tg_plane[32 * q : 32 * q + 4, :].bitcast(I32),
-                tg_scales[0, 4 * q : 4 * q + 4, :].bitcast(I32),
-            )
+        for q in range(3):
+            load_scales(q)
         for i in range(2, TILES):
             nc.sync.dma_start(x[i][:], xf_rows[i])
+        load_scales(3)
         nc.sync.dma_start(
             tg_codes[:].bitcast(I32), tg_words[0].rearrange("p n t -> p (n t)").bitcast(I32)
         )
@@ -72,17 +77,16 @@ def tile_list_moment_of_changes_kernel(tc, xf, rw, tg_words, tg_scales, old, off
             plus = held.tile([P, J], F32, name=f"plus{i}")
             nc.vector.tensor_scalar(minus[:], x[i][:].indirect(list2[:]), -1.0, 0.0, MULT, ADD)
             nc.vector.tensor_copy(plus[:], x[i][:].indirect(list1[:]))
-            banks = [psum.tile([P, P], F32, name=f"turned{i}_{t}", tag="ring", bufs=5) for t in range(PACK)]
+            banks = [psum.tile([P, P], F32, name=f"turned{i}_{t}", tag=f"ring{(i * PACK + t) % RING}") for t in range(PACK)]
             for t in range(PACK):
                 nc.tensor.matmul(banks[t][:], minus[:, t::PACK], ident[:], start=True, stop=False, is_transpose=True)
             for t in range(PACK):
                 nc.tensor.matmul(banks[t][:], plus[:, t::PACK], ident[:], start=False, stop=True, is_transpose=True)
                 nc.scalar.activation(grouped[:, :, t], banks[t][:], COPY, scale=rw_sb[:, t : t + 1])
 
-        def quantise(name, grouped, width, tag):
+        def quantise(name, grouped, width, tag, plane):
             codes = held.tile([P, width], U32, name=f"codes{name}", tag=tag, align_bytes=64)
-            plane = held.tile([P, width], U8, name=f"plane{name}", align_bytes=64)
-            nc.vector.quantize_mx(out=codes[:].bitcast(FP8X4), scales=plane[:], in_=grouped)
+            nc.vector.quantize_mx(out=codes[:].bitcast(FP8X4), scales=plane, in_=grouped)
             return codes, plane
 
         def multiply(acc, quantised, k_cols, n_cols):
@@ -107,6 +111,8 @@ def tile_list_moment_of_changes_kernel(tc, xf, rw, tg_words, tg_scales, old, off
             nc.vector.scalar_tensor_tensor(y[:], acc[:], 0.03, half_old[i][:, n_cols], MULT, ADD)
             queue.dma_start(out_rows[i][:, n_cols], y[:])
 
+        plane2 = held.tile([P, P], U8, name="plane2", align_bytes=64)
+        plane3 = held.tile([P, P], U8, name="plane3", align_bytes=64)
         all_n = slice(0, N)
         first_k = slice(0, P)
         grouped01 = held.tile([P, 2, P, PACK], BF16, name="grouped01", align_bytes=64)
@@ -114,17 +120,16 @@ def tile_list_moment_of_changes_kernel(tc, xf, rw, tg_words, tg_scales, old, off
         gather_and_turn(0, grouped01[:, 0])
         gather_and_turn(1, grouped01[:, 1])
         gather_and_turn(2, grouped2[:])
-        quantised01 = quantise("01", grouped01[:].rearrange("p i k t -> p (i k t)"), 2 * P, "window2")
-        acc01 = [psum.tile([P, N], F32, name=f"acc{i}") for i in range(2)]
-        for i in range(2):
-            multiply(acc01[i], quantised01, slice(i * P, (i + 1) * P), all_n)
-
         second = held.tile([P, J], F32, name="second")
         diff = held.tile([P, J], F32, name="diff")
         pairs = held.tile([P, 2, J // 2], BF16, name="pairs", align_bytes=64)
         halves = [slice(h * HALF, (h + 1) * HALF) for h in range(2)]
-        for h in range(2):
-            nc.vector.tensor_copy(second[:, halves[h]], x[last][:].indirect(list2[:, h * 16 : (h + 1) * 16]))
+        nc.vector.tensor_copy(second[:], x[last][:].indirect(list2[:]))
+        quantised01 = quantise("01", grouped01[:].rearrange("p i k t -> p (i k t)"), 2 * P, "codes01", tg_plane[4:P, 0 : 2 * P])
+        acc01 = [psum.tile([P, N], F32, name=f"acc{i}", tag=f"ring{2 + i}") for i in range(2)]
+        for i in range(2):
+            multiply(acc01[i], quantised01, slice(i * P, (i + 1) * P), all_n)
+
         for h in range(2):
             nc.vector.tensor_tensor(
                 diff[:, halves[h]], x[last][:].indirect(list1[:, h * 16 : (h + 1) * 16]), second[:, halves[h]], SUB
@@ -145,13 +150,13 @@ def tile_list_moment_of_changes_kernel(tc, xf, rw, tg_words, tg_scales, old, off
         nc.scalar.copy(grouped3[:].bitcast(F32), turned[:].rearrange("p u k -> p k u"))
         half_old.extend(halve(i) for i in range(2, TILES))
 
-        quantised2 = quantise("2", grouped2[:].rearrange("p k t -> p (k t)"), P, "window3")
-        acc2 = psum.tile([P, N], F32, name="acc2", tag="ring", bufs=5)
+        quantised2 = quantise("2", grouped2[:].rearrange("p k t -> p (k t)"), P, "window3", plane2[:])
+        acc2 = psum.tile([P, N], F32, name="acc2", tag="ring0")
         multiply(acc2, quantised2, first_k, all_n)
         finish(0, acc01[0], all_n, "y0", "y0", nc.sync)
         finish(1, acc01[1], all_n, "y1", "y1", nc.sync)
-        quantised3 = quantise("3", grouped3[:].rearrange("p k t -> p (k t)"), P, "half0")
-        acc3 = [psum.tile([P, N // 2], F32, name=f"acc3_{h}", tag="ring", bufs=5) for h in range(2)]
+        quantised3 = quantise("3", grouped3[:].rearrange("p k t -> p (k t)"), P, "half0", plane3[:])
+        acc3 = [psum.tile([P, N // 2], F32, name=f"acc3_{h}", tag=f"ring{5 + h}") for h in range(2)]
         for h in range(2):
             multiply(acc3[h], quantised3, first_k, halves[h])
         finish(2, acc2, all_n, "y2", "old1", nc.sync)

@@ -126,7 +126,7 @@ def tile_list_moment_of_changes_kernel(tc, xf, rw, tg_words, tg_scales, old, off
         halves = [slice(h * HALF, (h + 1) * HALF) for h in range(2)]
         nc.vector.tensor_copy(second[:], x[last][:].indirect(list2[:]))
         quantised01 = quantise("01", grouped01[:].rearrange("p i k t -> p (i k t)"), 2 * P, "codes01", tg_plane[4:P, 0 : 2 * P])
-        acc01 = [psum.tile([P, N], F32, name=f"acc{i}", tag=f"ring{2 + i}") for i in range(2)]
+        acc01 = [psum.tile([P, N], F32, name=f"acc{i}", tag=f"ring{5 + i}") for i in range(2)]
         for i in range(2):
             multiply(acc01[i], quantised01, slice(i * P, (i + 1) * P), all_n)
 
@@ -156,7 +156,7 @@ def tile_list_moment_of_changes_kernel(tc, xf, rw, tg_words, tg_scales, old, off
         finish(0, acc01[0], all_n, "y0", "y0", nc.sync)
         finish(1, acc01[1], all_n, "y1", "y1", nc.sync)
         quantised3 = quantise("3", grouped3[:].rearrange("p k t -> p (k t)"), P, "half0", plane3[:])
-        acc3 = [psum.tile([P, N // 2], F32, name=f"acc3_{h}", tag=f"ring{5 + h}") for h in range(2)]
+        acc3 = [psum.tile([P, N // 2], F32, name=f"acc3_{h}", tag=f"ring{1 + h}") for h in range(2)]
         for h in range(2):
             multiply(acc3[h], quantised3, first_k, halves[h])
         finish(2, acc2, all_n, "y2", "old1", nc.sync)

from contextlib import ExitStack

import concourse.mybir as mybir
from concourse.masks import make_identity

K, T, J, N = 512, 2048, 512, 512
FLOPS = 2 * K * J * N

F32 = mybir.dt.float32
BF16 = mybir.dt.bfloat16
I32 = mybir.dt.int32
U32 = mybir.dt.uint32
U16 = mybir.dt.uint16
U8 = mybir.dt.uint8
FP8X4 = mybir.dt.float8_e4m3fn_x4
COPY = mybir.ActivationFunctionType.Copy
MULT = mybir.AluOpType.mult
ADD = mybir.AluOpType.add
SUB = mybir.AluOpType.subtract

P = 128
PACK = 4
TILES = K // P
HALF = J // 2
RING = 7


def tile_list_moment_of_changes_kernel(tc, xf, rw, tg_words, tg_scales, old, offs, offs2, out):
    nc = tc.nc
    last = TILES - 1
    with ExitStack() as ctx:
        held = ctx.enter_context(tc.tile_pool(name="held", bufs=1))
        psum = ctx.enter_context(tc.psum_pool(name="psum", bufs=1))

        list1 = held.tile([P, J // 16], U16, name="list1")
        list2 = held.tile([P, J // 16], U16, name="list2")
        x = [held.tile([P, T], F32, name=f"x{i}", tag=f"window{i}", align_bytes=64) for i in range(TILES)]
        old_sb = [held.tile([P, N], F32, name=f"old{i}", tag=f"old{i}", align_bytes=64) for i in range(TILES)]
        rw_sb = held.tile([P, PACK], F32, name="rw_sb")
        tg_codes = held.tile([P, N], U32, name="tg_codes", align_bytes=64)
        tg_plane = held.tile([P, N], U8, name="tg_plane", align_bytes=64)
        ident = held.tile([P, P], F32, name="ident")

        xf_rows = xf.rearrange("(p i) t -> i p t", i=TILES)
        old_rows = old.rearrange("(p i) n -> p i n", i=TILES)
        out_rows = out.rearrange("(p i) n -> i p n", i=TILES)
        def load_scales(q):
            nc.sync.dma_start(
                tg_plane[32 * q : 32 * q + 4, :].bitcast(I32),
                tg_scales[0, 4 * q : 4 * q + 4, :].bitcast(I32),
            )

        nc.gpsimd.memset(tg_plane[:].bitcast(I32), 0)
        nc.sync.dma_start(x[0][:], xf_rows[0])
        nc.sync.dma_start(list2[:], offs2)
        nc.sync.dma_start(list1[:], offs)
        nc.sync.dma_start(rw_sb[:], rw.rearrange("o (p t) -> (o p) t", t=PACK))
        nc.sync.dma_start(x[1][:], xf_rows[1])
        for q in range(3):
            load_scales(q)
        for i in range(2, TILES):
            nc.sync.dma_start(x[i][:], xf_rows[i])
        load_scales(3)
        nc.sync.dma_start(
            tg_codes[:].bitcast(I32), tg_words[0].rearrange("p n t -> p (n t)").bitcast(I32)
        )
        for i in range(TILES):
            nc.sync.dma_start(old_sb[i][:], old_rows[:, i, :])
        make_identity(nc, ident[:])

        rw_wide = psum.tile([P, PACK, P], F32, name="rw_wide", tag="shared")
        for t in range(PACK):
            nc.tensor.transpose(rw_wide[:, t, :], rw_sb[:, t : t + 1].to_broadcast([P, P]), ident[:])

        def gather_and_turn(i, grouped):
            minus = held.tile([P, J], F32, name=f"minus{i}")
            plus = held.tile([P, J], F32, name=f"plus{i}")
            nc.vector.tensor_scalar(minus[:], x[i][:].indirect(list2[:]), -1.0, 0.0, MULT, ADD)
            nc.vector.tensor_copy(plus[:], x[i][:].indirect(list1[:]))
            banks = [psum.tile([P, P], F32, name=f"turned{i}_{t}", tag=f"ring{(i * PACK + t) % RING}") for t in range(PACK)]
            for t in range(PACK):
                nc.tensor.matmul(banks[t][:], minus[:, t::PACK], ident[:], start=True, stop=False, is_transpose=True)
            for t in range(PACK):
                nc.tensor.matmul(banks[t][:], plus[:, t::PACK], ident[:], start=False, stop=True, is_transpose=True)
                nc.scalar.activation(grouped[:, :, t], banks[t][:], COPY, scale=rw_sb[:, t : t + 1])

        def quantise(name, grouped, width, tag, plane):
            codes = held.tile([P, width], U32, name=f"codes{name}", tag=tag, align_bytes=64)
            nc.vector.quantize_mx(out=codes[:].bitcast(FP8X4), scales=plane, in_=grouped)
            return codes, plane

        def multiply(acc, quantised, k_cols, n_cols):
            codes, plane = quantised
            nc.tensor.matmul_mx(
                out=acc[:],
                lhsT=codes[:, k_cols].bitcast(FP8X4),
                lhsT_scale=plane[:, k_cols],
                rhs=tg_codes[:, n_cols].bitcast(FP8X4),
                rhs_scale=tg_plane[:, n_cols],
                start=True,
                stop=True,
            )

        def halve(i):
            half = held.tile([P, N], F32, name=f"half{i}", tag=f"half{i}", align_bytes=64)
            nc.scalar.activation(half[:], old_sb[i][:], COPY, scale=0.5)
            return half

        def finish(i, acc, n_cols, name, tag, queue):
            y = held.tile([P, n_cols.stop - n_cols.start], F32, name=name, tag=tag, align_bytes=64)
            nc.vector.scalar_tensor_tensor(y[:], acc[:], 0.03, half_old[i][:, n_cols], MULT, ADD)
            queue.dma_start(out_rows[i][:, n_cols], y[:])

        plane2 = held.tile([P, P], U8, name="plane2", align_bytes=64)
        plane3 = held.tile([P, P], U8, name="plane3", align_bytes=64)
        all_n = slice(0, N)
        first_k = slice(0, P)
        grouped01 = held.tile([P, 2, P, PACK], BF16, name="grouped01", align_bytes=64)
        grouped2 = held.tile([P, P, PACK], BF16, name="grouped2", align_bytes=64)
        gather_and_turn(0, grouped01[:, 0])
        gather_and_turn(1, grouped01[:, 1])
        gather_and_turn(2, grouped2[:])
        second = held.tile([P, J], F32, name="second")
        diff = held.tile([P, J], F32, name="diff")
        pairs = held.tile([P, 2, J // 2], BF16, name="pairs", align_bytes=64)
        halves = [slice(h * HALF, (h + 1) * HALF) for h in range(2)]
        nc.vector.tensor_copy(second[:], x[last][:].indirect(list2[:]))
        quantised01 = quantise("01", grouped01[:].rearrange("p i k t -> p (i k t)"), 2 * P, "codes01", tg_plane[4:P, 0 : 2 * P])
        acc01 = [psum.tile([P, N], F32, name=f"acc{i}", tag=f"ring{5 + i}") for i in range(2)]
        for i in range(2):
            multiply(acc01[i], quantised01, slice(i * P, (i + 1) * P), all_n)

        for h in range(2):
            nc.vector.tensor_tensor(
                diff[:, halves[h]], x[last][:].indirect(list1[:, h * 16 : (h + 1) * 16]), second[:, halves[h]], SUB
            )
        for h in range(2):
            q_cols = slice(h * 64, (h + 1) * 64)
            nc.vector.tensor_tensor(
                pairs[:].rearrange("p u (q e) -> p u q e", e=2)[:, :, q_cols, :],
                diff[:, halves[h]].rearrange("p (q u e) -> p u q e", u=2, e=2),
                rw_wide[:].rearrange("p (u e) q -> p u q e", e=2)[:, :, q_cols, :],
                MULT,
            )
        turned = psum.tile([P, 2, P], F32, name="turned_pairs", tag="shared")
        for u in range(2):
            nc.tensor.transpose(turned[:, u, :], pairs[:].bitcast(F32)[:, u, :], ident[:])
        half_old = [halve(i) for i in range(2)]
        grouped3 = held.tile([P, P, PACK], BF16, name="grouped3", tag="old1", align_bytes=64)
        nc.scalar.copy(grouped3[:].bitcast(F32), turned[:].rearrange("p u k -> p k u"))
        half_old.extend(halve(i) for i in range(2, TILES))

        quantised2 = quantise("2", grouped2[:].rearrange("p k t -> p (k t)"), P, "window3", plane2[:])
        acc2 = psum.tile([P, N], F32, name="acc2", tag="ring0")
        multiply(acc2, quantised2, first_k, all_n)
        finish(0, acc01[0], all_n, "y0", "y0", nc.sync)
        finish(1, acc01[1], all_n, "y1", "y1", nc.sync)
        quantised3 = quantise("3", grouped3[:].rearrange("p k t -> p (k t)"), P, "half0", plane3[:])
        acc3 = [psum.tile([P, N // 2], F32, name=f"acc3_{h}", tag=f"ring{1 + h}") for h in range(2)]
        for h in range(2):
            multiply(acc3[h], quantised3, first_k, halves[h])
        finish(2, acc2, all_n, "y2", "old1", nc.sync)
        finish(last, acc3[0], halves[0], "y3a", "y3a", nc.sync)
        finish(last, acc3[1], halves[1], "y3b", "y3b", nc.scalar)
